import numpy as np
import ml_dtypes


def mxq(x, axis, fmt="e4m3"):
    dtype, down = {"e4m3": (ml_dtypes.float8_e4m3fn, 7), "e5m2": (ml_dtypes.float8_e5m2, 14)}[fmt]
    v = np.moveaxis(np.asarray(x, np.float32).astype(ml_dtypes.bfloat16).astype(np.float64), axis, -1)
    blocks = v.reshape(v.shape[:-1] + (-1, 32))
    amax = np.abs(blocks).max(-1, keepdims=True)
    byte = np.maximum(np.where(amax > 0, np.frexp(amax)[1] - 1 + 127, 0) - down, 1)
    scale = np.exp2(byte - 127.0)
    codes = (blocks / scale).astype(np.float32).astype(dtype).astype(np.float64)
    return np.moveaxis((codes * scale).reshape(v.shape), -1, axis)


WIDE = False


def mx_kscale(k):
    if not WIDE:
        return np.ones(k)
    levels = np.array([10, -10, 5, -5, 0])
    if k % 512:
        return np.exp2(np.random.permutation(np.resize(levels, k // 32))).repeat(32)
    a = np.empty((k // 512, 16))
    for p in range(k // 512):
        a[p, :8] = np.random.permutation(np.resize(levels, 8))
        for g in range(8):
            far = levels[np.abs(levels - a[p, g]) >= 10]
            a[p, g + 8] = far[np.random.randint(len(far))]
    return np.exp2(a.ravel()).repeat(32)


def f64(x):
    return np.asarray(x).astype(np.float64)


def striped(idx):
    return np.tile(idx.reshape(-1, 16).T, (8, 1)).astype(np.uint16)


def unstriped(offs):
    return offs[:16].T.reshape(-1).astype(np.int64)


def striped8(idx):
    return np.concatenate([x.reshape(-1, 16).T for x in idx]).astype(np.uint16)


def runs(offs, k):
    lists = np.stack([offs[16 * r : 16 * r + 16].T.reshape(-1) for r in range(8)]).astype(np.int64)
    return lists[np.arange(k) % 512 // 64]


def pack_weight(w):
    k, n = w.shape
    w = f64(np.asarray(w, np.float32).astype(ml_dtypes.bfloat16)).reshape(k // 32, 32, n)
    amax = np.abs(w).max(1)
    byte = np.clip(np.where(amax > 0, np.frexp(amax)[1] - 1 + 127 - 7, 1), 1, 254)
    scaled = (w * np.exp2(127.0 - byte)[:, None, :]).reshape(k, n).astype(np.float32)
    words = np.ascontiguousarray(scaled.reshape(k // 512, 128, 4, n).transpose(0, 1, 3, 2)).astype(ml_dtypes.float8_e4m3fn).view(np.uint8)
    return words, np.ascontiguousarray(byte.astype(np.uint8).reshape(k // 512, 16, n))


def unpack_weight(words, scales):
    g, p, n, _ = words.shape
    vals = np.ascontiguousarray(words).view(ml_dtypes.float8_e4m3fn).astype(np.float64) * np.repeat(np.exp2(scales.astype(np.float64) - 127.0), 8, axis=1)[..., None]
    return vals.transpose(0, 1, 3, 2).reshape(g * 512, n)


K, T, S, N, H = 512, 2048, 512, 512, 512


def setup_inputs():
    n = np.random.standard_normal
    s = mx_kscale(K)[:, None]
    u = mx_kscale(H)
    packed_xT = pack_weight(n((K, T)) * s)
    return {
        "x_words": packed_xT[0],
        "x_scales": packed_xT[1],
        "w1": (n((K, H)) / np.sqrt(2 * K) / s).astype(np.float32),
        "w2": (n((K, H)) / np.sqrt(2 * K) / s).astype(np.float32),
        "gn": (np.random.uniform(0.5, 1.5, (H, 1)) * u[:, None]).astype(np.float32),
        "w3": (n((H, N)) / np.sqrt(H) / u[:, None]).astype(np.float32),
        "offs": striped(np.random.permutation(T)[:S]),
        "c1": striped(np.random.permutation(T)[:S]),
        "c2": striped(np.random.permutation(T)[:S]),
        "mate": striped8(np.stack([np.random.permutation(S) for _ in range(8)])),
    }


def reference(x_words, x_scales, w1, w2, gn, w3, offs, c1, c2, mate):
    xq = unpack_weight(x_words, x_scales)[:, unstriped(offs)]
    x_c1 = unpack_weight(x_words, x_scales)[:, unstriped(c1)]
    w1q = mxq(f64(w1), 0, "e4m3")
    w2q = mxq(f64(w2), 0, "e4m3")
    y = w1q.T @ xq + w2q.T @ x_c1
    x_c2 = unpack_weight(x_words, x_scales)[:, unstriped(c2)]
    e = w1q.T @ x_c1 + w2q.T @ x_c2
    mx = np.tanh(np.maximum(y, e))
    z = f64(gn) * (mx + mx[np.arange(H)[:, None], runs(mate, H)])
    return mxq(f64(w3), 0, "e4m3").T @ mxq(z, 0, "e4m3")

@@ -1,0 +1,204 @@
+from contextlib import ExitStack
+
+import concourse.mybir as mybir
+
+K, T, S, N, H = 512, 2048, 512, 512, 512
+FLOPS = 2 * S * (4 * K * H + H * N)
+
+F32 = mybir.dt.float32
+BF16 = mybir.dt.bfloat16
+I32 = mybir.dt.int32
+U32 = mybir.dt.uint32
+U16 = mybir.dt.uint16
+U8 = mybir.dt.uint8
+FP8X4 = mybir.dt.float8_e4m3fn_x4
+ALU = mybir.AluOpType
+ACT = mybir.ActivationFunctionType
+
+P = 128
+PACK = 4
+LIST_ROWS = 16
+CHUNKS = ((0, 128), (128, 128), (256, 128), (384, 128))
+EARLY_WORDS = 512
+HALF = S // 2
+
+
+def tile_picked_charcnn_tanh_p_kernel(
+    tc, x_words, x_scales, w1, w2, gn, w3, offs, c1, c2, mate, out
+):
+    nc = tc.nc
+    with ExitStack() as ctx:
+        keep = ctx.enter_context(tc.tile_pool(name="keep", bufs=1))
+        psum = ctx.enter_context(tc.psum_pool(name="psum", bufs=1))
+
+        def load_list(name, src):
+            tile = keep.tile([P, S // LIST_ROWS], U16, name=name)
+            nc.sync.dma_start(tile[:], src)
+            return tile
+
+        def load_weight(name, src):
+            tile = keep.tile([P, PACK, src.shape[1]], F32, name=name)
+            nc.sync.dma_start(tile[:], src.rearrange("(p j) c -> p j c", j=PACK))
+            return tile
+
+        table_scales = keep.tile([P, T], U8, name="table_scales")
+        nc.vector.memset(table_scales[:].bitcast(I32), 0)
+        table_words = keep.tile([P, T], I32, name="table_words")
+        words_hbm = x_words[0].rearrange("p n t -> p (n t)").bitcast(I32)
+        lists = [load_list("offs_list", offs), load_list("c1_list", c1)]
+        nc.sync.dma_start(table_words[:, :EARLY_WORDS], words_hbm[:, :EARLY_WORDS])
+        for q in range(4):
+            nc.sync.dma_start(
+                table_scales[32 * q : 32 * q + 4, :].bitcast(I32),
+                x_scales[0, 4 * q : 4 * q + 4, :].bitcast(I32),
+            )
+        warm_in = keep.tile([P, 1], F32, name="warm_in")
+        warm_out = keep.tile([P, 1], F32, name="warm_out")
+        nc.vector.memset(warm_in[:], 0.0)
+        nc.scalar.activation(warm_out[:], warm_in[:], ACT.Tanh)
+
+        nc.sync.dma_start(table_words[:, EARLY_WORDS:], words_hbm[:, EARLY_WORDS:])
+        lists.append(load_list("c2_list", c2))
+        w1_raw = load_weight("w1_raw", w1)
+        w2_raw = load_weight("w2_raw", w2)
+        w3_raw = [load_weight(f"w3_raw{h}", w3[:, HALF * h : HALF * h + HALF]) for h in range(2)]
+        mate_list = load_list("mate_list", mate)
+        gain = keep.tile([P, PACK], F32, name="gain")
+        nc.sync.dma_start(gain[:], gn.rearrange("(p t) o -> p (t o)", t=PACK))
+
+        x_sc = [keep.tile([P, S], U8, name=f"x_sc{i}", align_bytes=64) for i in range(3)]
+
+        def gather_scales(i):
+            nc.vector.tensor_copy(x_sc[i][:], table_scales[:].indirect(lists[i][:]))
+
+        def gather_words(i):
+            nc.vector.tensor_copy(x_cd[i][:], table_words[:].bitcast(U32).indirect(lists[i][:]))
+
+        def deal_pair(name, raw, u):
+            grouped = keep.tile([P, 2, P, PACK], BF16, name=name, tag=name, align_bytes=64)
+            nc.scalar.copy(
+                grouped[:].rearrange("p e m j -> p m j e"),
+                raw[:].rearrange("p j (m u e) -> p u m j e", u=2, e=2)[:, u],
+            )
+            return grouped
+
+        def quantize(name, grouped_flat, width, tag=None):
+            codes = keep.tile([P, width], U32, name=name + "_cd", tag=tag or name + "_cd", align_bytes=64)
+            scales = keep.tile([P, width], U8, name=name + "_sc", align_bytes=64)
+            nc.vector.quantize_mx(codes[:].bitcast(FP8X4), scales[:], grouped_flat)
+            return codes, scales
+
+        def mm(acc, w, cols, x_codes, x_scale, start, stop):
+            nc.tensor.matmul_mx(
+                out=acc,
+                lhsT=w[0][:, cols].bitcast(FP8X4),
+                lhsT_scale=w[1][:, cols],
+                rhs=x_codes.bitcast(FP8X4),
+                rhs_scale=x_scale,
+                start=start,
+                stop=stop,
+            )
+
+        def both(grouped):
+            return grouped[:].rearrange("p e m j -> p (e m j)")
+
+        def one(grouped, e):
+            return grouped[:, e, :, :].rearrange("p m j -> p (m j)")
+
+        w1_g = [deal_pair(f"w1_g{u}", w1_raw, u) for u in range(2)]
+        w2_g = [deal_pair(f"w2_g{u}", w2_raw, u) for u in range(2)]
+
+        x_cd = [keep.tile([P, S], U32, name=f"x_cd{i}", align_bytes=64) for i in range(2)]
+        for i in range(3):
+            gather_scales(i)
+        gather_words(0)
+        gather_words(1)
+        w1_q = [quantize("w1_0", both(w1_g[0]), 2 * P)]
+        x_cd.append(keep.tile([P, S], U32, name="x_cd2", tag="w1_g0", align_bytes=64))
+        gather_words(2)
+        w2_q = [quantize(f"w2_{e}", one(w2_g[0], e), P) for e in range(2)]
+        w1_q.append(quantize("w1_1", both(w1_g[1]), 2 * P, tag="w2_g0"))
+        w2_q.extend(quantize(f"w2_{2 + e}", one(w2_g[1], e), P) for e in range(2))
+
+        y_acc = [psum.tile([P, S], F32, name=f"y{t}", tag=f"bank{2 * t}") for t in range(PACK)]
+        e_acc = [psum.tile([P, S], F32, name=f"e{t}", tag=f"bank{2 * t + 1}") for t in range(PACK)]
+
+        def first_pass(t):
+            cols = slice(P * (t % 2), P * (t % 2) + P)
+            mm(y_acc[t][:], w1_q[t // 2], cols, x_cd[0][:], x_sc[0][:], True, False)
+            mm(e_acc[t][:], w1_q[t // 2], cols, x_cd[1][:], x_sc[1][:], True, False)
+
+        def second_pass(t):
+            mm(e_acc[t][:], w2_q[t], slice(0, P), x_cd[2][:], x_sc[2][:], False, True)
+            mm(y_acc[t][:], w2_q[t], slice(0, P), x_cd[1][:], x_sc[1][:], False, True)
+
+        first_pass(0)
+        first_pass(1)
+        second_pass(0)
+        second_pass(1)
+        for t in (2, 3):
+            first_pass(t)
+            second_pass(t)
+
+        own = keep.tile([P, PACK, S], F32, name="own")
+        fetched = keep.tile([P, PACK, S], F32, name="fetched")
+        window = [keep.tile([P, S], F32, name=f"window{t}") for t in range(PACK)]
+        e_sb = [keep.tile([P, S], F32, name=f"e_sb{t}") for t in range(PACK)]
+        larger = [keep.tile([P, S], F32, name=f"larger{t}") for t in range(PACK)]
+        mx = [keep.tile([P, S], F32, name=f"mx{t}", tag=f"mx{t}", align_bytes=64) for t in range(PACK)]
+
+        def take_larger(t):
+            nc.scalar.copy(e_sb[t][:], e_acc[t][:])
+            nc.vector.tensor_tensor(larger[t][:], y_acc[t][:], e_sb[t][:], ALU.max)
+
+        def activate_and_fetch(t):
+            nc.scalar.activation(mx[t][:], larger[t][:], ACT.Tanh)
+            nc.scalar.activation(window[t][:], mx[t][:], ACT.Copy, scale=gain[:, t : t + 1])
+            for j0 in (0, HALF):
+                cols = slice(j0 // LIST_ROWS, (j0 + HALF) // LIST_ROWS)
+                nc.vector.tensor_copy(
+                    fetched[:, t, j0 : j0 + HALF], window[t][:].indirect(mate_list[:, cols])
+                )
+
+        def group_w3(h, copy, tag):
+            grouped = keep.tile([P, HALF, PACK], BF16, name=f"w3_g{h}", tag=tag, align_bytes=64)
+            copy(
+                grouped[:].rearrange("p (c i) j -> p c j i", i=4),
+                w3_raw[h][:].rearrange("p j (c i) -> p c j i", i=4),
+            )
+            return quantize(f"w3_{h}", grouped[:].rearrange("p c j -> p (c j)"), HALF)
+
+        w3_q = [group_w3(0, nc.vector.tensor_copy, "w2_g1")]
+        take_larger(0)
+        take_larger(1)
+        activate_and_fetch(0)
+        take_larger(2)
+        activate_and_fetch(1)
+        take_larger(3)
+        activate_and_fetch(2)
+        activate_and_fetch(3)
+        for j0 in (0, HALF):
+            for t in range(PACK):
+                nc.scalar.copy(own[:, t, j0 : j0 + HALF], window[t][:, j0 : j0 + HALF])
+        w3_q.append(group_w3(1, nc.scalar.copy, "mx3"))
+
+        out_rows = out.rearrange("(r p) j -> p r j", p=P)
+        for c, (j0, n) in enumerate(CHUNKS):
+            z = keep.tile([P, n, PACK], BF16, name=f"z{c}", align_bytes=64)
+            nc.vector.tensor_tensor(
+                z[:].rearrange("p (c i) t -> p c t i", i=4),
+                own[:, :, j0 : j0 + n].rearrange("p t (c i) -> p c t i", i=4),
+                fetched[:, :, j0 : j0 + n].rearrange("p t (c i) -> p c t i", i=4),
+                ALU.add,
+            )
+            z_q = quantize(f"z{c}", z[:].rearrange("p c t -> p (c t)"), n)
+            for h in range(2):
+                acc = psum.tile([P, 2, n], F32, name=f"o{c}_{h}", tag=f"bank{2 * c + h}")
+                for r in range(2):
+                    mm(acc[:, r, :], w3_q[h], slice(P * r, P * r + P), z_q[0][:], z_q[1][:], True, True)
+                res = keep.tile([P, 2, n], F32, name=f"res{c}_{h}")
+                if c >= len(CHUNKS) - 2 and h == 1:
+                    nc.vector.tensor_copy(res[:], acc[:])
+                else:
+                    nc.scalar.copy(res[:], acc[:])
+                nc.sync.dma_start(out_rows[:, 2 * h : 2 * h + 2, j0 : j0 + n], res[:])

@@ -18,7 +18,7 @@ ACT = mybir.ActivationFunctionType
 P = 128
 PACK = 4
 LIST_ROWS = 16
-CHUNKS = ((0, 128), (128, 128), (256, 128), (384, 128))
+CHUNK = 128
 EARLY_WORDS = 512
 HALF = S // 2
 
@@ -61,7 +61,7 @@ def tile_picked_charcnn_tanh_p_kernel(
         lists.append(load_list("c2_list", c2))
         w1_raw = load_weight("w1_raw", w1)
         w2_raw = load_weight("w2_raw", w2)
-        w3_raw = [load_weight(f"w3_raw{h}", w3[:, HALF * h : HALF * h + HALF]) for h in range(2)]
+        w3_raw = load_weight("w3_raw", w3)
         mate_list = load_list("mate_list", mate)
         gain = keep.tile([P, PACK], F32, name="gain")
         nc.sync.dma_start(gain[:], gn.rearrange("(p t) o -> p (t o)", t=PACK))
@@ -132,6 +132,8 @@ def tile_picked_charcnn_tanh_p_kernel(
             mm(e_acc[t][:], w2_q[t], slice(0, P), x_cd[2][:], x_sc[2][:], False, True)
             mm(y_acc[t][:], w2_q[t], slice(0, P), x_cd[1][:], x_sc[1][:], False, True)
 
+        for rep in range(3):
+            mm(y_acc[3][:], (x_cd[0], x_sc[0]), slice(0, P), x_cd[0][:], x_sc[0][:], True, True)
         first_pass(0)
         first_pass(1)
         second_pass(0)
@@ -141,64 +143,72 @@ def tile_picked_charcnn_tanh_p_kernel(
             second_pass(t)
 
         own = keep.tile([P, PACK, S], F32, name="own")
-        fetched = keep.tile([P, PACK, S], F32, name="fetched")
         window = [keep.tile([P, S], F32, name=f"window{t}") for t in range(PACK)]
-        e_sb = [keep.tile([P, S], F32, name=f"e_sb{t}") for t in range(PACK)]
-        larger = [keep.tile([P, S], F32, name=f"larger{t}") for t in range(PACK)]
-        mx = [keep.tile([P, S], F32, name=f"mx{t}", tag=f"mx{t}", align_bytes=64) for t in range(PACK)]
+        e_sb = [keep.tile([P, S], F32, name=f"e_sb{t}", tag=f"e_sb{t}", align_bytes=64) for t in range(PACK)]
+        larger = [keep.tile([P, S], F32, name=f"larger{t}", tag=f"larger{t}", align_bytes=64) for t in range(PACK)]
+        mx = [keep.tile([P, S], F32, name=f"mx{t}", tag=f"mx{t}") for t in range(PACK)]
+        early = keep.tile([P, PACK, HALF], F32, name="early")
 
         def take_larger(t):
             nc.scalar.copy(e_sb[t][:], e_acc[t][:])
             nc.vector.tensor_tensor(larger[t][:], y_acc[t][:], e_sb[t][:], ALU.max)
 
-        def activate_and_fetch(t):
-            nc.scalar.activation(mx[t][:], larger[t][:], ACT.Tanh)
-            nc.scalar.activation(window[t][:], mx[t][:], ACT.Copy, scale=gain[:, t : t + 1])
-            for j0 in (0, HALF):
-                cols = slice(j0 // LIST_ROWS, (j0 + HALF) // LIST_ROWS)
-                nc.vector.tensor_copy(
-                    fetched[:, t, j0 : j0 + HALF], window[t][:].indirect(mate_list[:, cols])
-                )
-
-        def group_w3(h, copy, tag):
-            grouped = keep.tile([P, HALF, PACK], BF16, name=f"w3_g{h}", tag=tag, align_bytes=64)
-            copy(
-                grouped[:].rearrange("p (c i) j -> p c j i", i=4),
-                w3_raw[h][:].rearrange("p j (c i) -> p c j i", i=4),
+        def add_mates(dst, t, j0, n):
+            cols = slice(j0 // LIST_ROWS, (j0 + n) // LIST_ROWS)
+            nc.vector.tensor_tensor(
+                dst, window[t][:].indirect(mate_list[:, cols]), own[:, t, j0 : j0 + n], ALU.add
             )
+
+        def activate(t):
+            nc.scalar.activation(mx[t][:], larger[t][:], ACT.Tanh)
+            nc.scalar.activation(own[:, t, :], mx[t][:], ACT.Copy, scale=gain[:, t : t + 1])
+            nc.vector.tensor_scalar(window[t][:], mx[t][:], gain[:, t : t + 1], None, ALU.mult)
+            add_mates(early[:, t, :], t, 0, HALF)
+
+        def group_w3(h, tag, copy, parts):
+            grouped = keep.tile([P, HALF, PACK], BF16, name=f"w3_g{h}", tag=tag, align_bytes=64)
+            dst = grouped[:].rearrange("p (c i) j -> p c j i", i=4)
+            src = w3_raw[:, :, HALF * h : HALF * h + HALF].rearrange("p j (c i) -> p c j i", i=4)
+            step = HALF // 4 // parts
+            for c0 in range(0, HALF // 4, step):
+                copy(dst[:, c0 : c0 + step], src[:, c0 : c0 + step])
             return quantize(f"w3_{h}", grouped[:].rearrange("p c j -> p (c j)"), HALF)
 
-        w3_q = [group_w3(0, nc.vector.tensor_copy, "w2_g1")]
+        w3_q = [group_w3(0, "w2_g1", nc.vector.tensor_copy, 1)]
         take_larger(0)
         take_larger(1)
-        activate_and_fetch(0)
+        activate(0)
         take_larger(2)
-        activate_and_fetch(1)
+        activate(1)
         take_larger(3)
-        activate_and_fetch(2)
-        activate_and_fetch(3)
-        for j0 in (0, HALF):
-            for t in range(PACK):
-                nc.scalar.copy(own[:, t, j0 : j0 + HALF], window[t][:, j0 : j0 + HALF])
-        w3_q.append(group_w3(1, nc.scalar.copy, "mx3"))
-
+        activate(2)
+        activate(3)
+        w3_q.append(group_w3(1, "larger3", nc.scalar.copy, 1))
         out_rows = out.rearrange("(r p) j -> p r j", p=P)
-        for c, (j0, n) in enumerate(CHUNKS):
-            z = keep.tile([P, n, PACK], BF16, name=f"z{c}", align_bytes=64)
-            nc.vector.tensor_tensor(
+
+        def finish(c, sums, weave, second_copy):
+            z = keep.tile([P, CHUNK, PACK], BF16, name=f"z{c}", tag=f"z{c}", align_bytes=64)
+            weave(
                 z[:].rearrange("p (c i) t -> p c t i", i=4),
-                own[:, :, j0 : j0 + n].rearrange("p t (c i) -> p c t i", i=4),
-                fetched[:, :, j0 : j0 + n].rearrange("p t (c i) -> p c t i", i=4),
-                ALU.add,
+                sums.rearrange("p t (c i) -> p c t i", i=4),
             )
-            z_q = quantize(f"z{c}", z[:].rearrange("p c t -> p (c t)"), n)
-            for h in range(2):
-                acc = psum.tile([P, 2, n], F32, name=f"o{c}_{h}", tag=f"bank{2 * c + h}")
+            z_q = quantize(f"z{c}", z[:].rearrange("p c t -> p (c t)"), CHUNK)
+            for h, copy in enumerate((nc.scalar.copy, second_copy)):
+                acc = psum.tile([P, 2, CHUNK], F32, name=f"o{c}_{h}", tag=f"bank{2 * c + h}")
                 for r in range(2):
                     mm(acc[:, r, :], w3_q[h], slice(P * r, P * r + P), z_q[0][:], z_q[1][:], True, True)
-                res = keep.tile([P, 2, n], F32, name=f"res{c}_{h}")
-                if c >= len(CHUNKS) - 2 and h == 1:
-                    nc.vector.tensor_copy(res[:], acc[:])
-                else:
-                    nc.scalar.copy(res[:], acc[:])
-                nc.sync.dma_start(out_rows[:, 2 * h : 2 * h + 2, j0 : j0 + n], res[:])
+                res = keep.tile([P, 2, CHUNK], F32, name=f"res{c}_{h}")
+                copy(res[:], acc[:])
+                nc.sync.dma_start(out_rows[:, 2 * h : 2 * h + 2, CHUNK * c : CHUNK * c + CHUNK], res[:])
+
+        finish(0, early[:, :, :CHUNK], nc.scalar.copy, nc.scalar.copy)
+        finish(1, early[:, :, CHUNK:], nc.scalar.copy, nc.scalar.copy)
+        late = [
+            keep.tile([P, PACK, CHUNK], F32, name="late0", tag="mx3"),
+            keep.tile([P, PACK, CHUNK], F32, name="late1", tag="z0", align_bytes=64),
+        ]
+        for c in range(2):
+            for t in range(PACK):
+                add_mates(late[c][:, t, :], t, HALF + CHUNK * c, CHUNK)
+        finish(2, late[0][:], nc.scalar.copy, nc.scalar.copy)
+        finish(3, late[1][:], nc.vector.tensor_copy, nc.vector.tensor_copy)

@@ -17,10 +17,11 @@ ACT = mybir.ActivationFunctionType
 
 P = 128
 PACK = 4
-LIST_ROWS = 16
-CHUNK = 128
-EARLY_WORDS = 512
+QUADRANT = 32
+LIST_GROUP = 16
+LINE = 4
 HALF = S // 2
+CHUNK = S // 4
 
 
 def tile_picked_charcnn_tanh_p_kernel(
@@ -32,183 +33,181 @@ def tile_picked_charcnn_tanh_p_kernel(
         psum = ctx.enter_context(tc.psum_pool(name="psum", bufs=1))
 
         def load_list(name, src):
-            tile = keep.tile([P, S // LIST_ROWS], U16, name=name)
+            tile = keep.tile([P, S // LIST_GROUP], U16, name=name)
             nc.sync.dma_start(tile[:], src)
             return tile
 
-        def load_weight(name, src):
-            tile = keep.tile([P, PACK, src.shape[1]], F32, name=name)
-            nc.sync.dma_start(tile[:], src.rearrange("(p j) c -> p j c", j=PACK))
+        def weight_rows(w):
+            return w.rearrange("(p j) c -> p j c", j=PACK)
+
+        def load_weight(name, w):
+            tile = keep.tile([P, PACK, w.shape[1]], F32, name=name)
+            nc.sync.dma_start(tile[:], weight_rows(w))
             return tile
 
         table_scales = keep.tile([P, T], U8, name="table_scales")
         nc.vector.memset(table_scales[:].bitcast(I32), 0)
-        table_words = keep.tile([P, T], I32, name="table_words")
-        words_hbm = x_words[0].rearrange("p n t -> p (n t)").bitcast(I32)
+
+        zero = keep.tile([P, 1], F32, name="zero")
+        no_bias = keep.tile([P, 1], F32, name="no_bias")
+        nc.vector.memset(zero[:], 0.0)
+        nc.scalar.activation(no_bias[:], zero[:], ACT.Tanh)
+
         lists = [load_list("offs_list", offs), load_list("c1_list", c1)]
-        nc.sync.dma_start(table_words[:, :EARLY_WORDS], words_hbm[:, :EARLY_WORDS])
-        for q in range(4):
+        w1_raw = keep.tile([P, PACK, H], F32, name="w1_raw")
+        nc.sync.dma_start(w1_raw[:, :1], weight_rows(w1)[:, :1])
+        for q in range(P // QUADRANT):
             nc.sync.dma_start(
-                table_scales[32 * q : 32 * q + 4, :].bitcast(I32),
+                table_scales[QUADRANT * q : QUADRANT * q + 4, :].bitcast(I32),
                 x_scales[0, 4 * q : 4 * q + 4, :].bitcast(I32),
             )
-        warm_in = keep.tile([P, 1], F32, name="warm_in")
-        warm_out = keep.tile([P, 1], F32, name="warm_out")
-        nc.vector.memset(warm_in[:], 0.0)
-        nc.scalar.activation(warm_out[:], warm_in[:], ACT.Tanh)
-
-        nc.sync.dma_start(table_words[:, EARLY_WORDS:], words_hbm[:, EARLY_WORDS:])
+        nc.sync.dma_start(w1_raw[:, 1:], weight_rows(w1)[:, 1:])
         lists.append(load_list("c2_list", c2))
-        w1_raw = load_weight("w1_raw", w1)
+        table_words = keep.tile([P, T], I32, name="table_words")
+        nc.sync.dma_start(table_words[:], x_words[0].rearrange("p n j -> p (n j)").bitcast(I32))
         w2_raw = load_weight("w2_raw", w2)
         w3_raw = load_weight("w3_raw", w3)
         mate_list = load_list("mate_list", mate)
         gain = keep.tile([P, PACK], F32, name="gain")
         nc.sync.dma_start(gain[:], gn.rearrange("(p t) o -> p (t o)", t=PACK))
 
-        x_sc = [keep.tile([P, S], U8, name=f"x_sc{i}", align_bytes=64) for i in range(3)]
-
-        def gather_scales(i):
-            nc.vector.tensor_copy(x_sc[i][:], table_scales[:].indirect(lists[i][:]))
-
-        def gather_words(i):
-            nc.vector.tensor_copy(x_cd[i][:], table_words[:].bitcast(U32).indirect(lists[i][:]))
-
         def deal_pair(name, raw, u):
-            grouped = keep.tile([P, 2, P, PACK], BF16, name=name, tag=name, align_bytes=64)
+            dealt = keep.tile([P, 2, P, PACK], BF16, name=name, tag=name, align_bytes=64)
             nc.scalar.copy(
-                grouped[:].rearrange("p e m j -> p m j e"),
+                dealt[:].rearrange("p e m j -> p m j e"),
                 raw[:].rearrange("p j (m u e) -> p u m j e", u=2, e=2)[:, u],
             )
-            return grouped
+            return dealt
 
-        def quantize(name, grouped_flat, width, tag=None):
-            codes = keep.tile([P, width], U32, name=name + "_cd", tag=tag or name + "_cd", align_bytes=64)
-            scales = keep.tile([P, width], U8, name=name + "_sc", align_bytes=64)
-            nc.vector.quantize_mx(codes[:].bitcast(FP8X4), scales[:], grouped_flat)
-            return codes, scales
+        def quantize(name, values, width, tag=None):
+            words = keep.tile([P, width], U32, name=name + "_words", tag=tag or name + "_words", align_bytes=64)
+            scales = keep.tile([P, width], U8, name=name + "_scales", align_bytes=64)
+            nc.vector.quantize_mx(words[:].bitcast(FP8X4), scales[:], values)
+            return words, scales
 
-        def mm(acc, w, cols, x_codes, x_scale, start, stop):
+        def quantize_pair(name, dealt, tag=None):
+            return quantize(name, dealt[:].rearrange("p e m j -> p (e m j)"), 2 * P, tag)
+
+        def quantize_plane(name, dealt, e):
+            return quantize(name, dealt[:, e, :, :].rearrange("p m j -> p (m j)"), P)
+
+        def product(acc, weights, block, moving, start, stop):
+            cols = slice(P * block, P * block + P)
             nc.tensor.matmul_mx(
                 out=acc,
-                lhsT=w[0][:, cols].bitcast(FP8X4),
-                lhsT_scale=w[1][:, cols],
-                rhs=x_codes.bitcast(FP8X4),
-                rhs_scale=x_scale,
+                lhsT=weights[0][:, cols].bitcast(FP8X4),
+                lhsT_scale=weights[1][:, cols],
+                rhs=moving[0].bitcast(FP8X4),
+                rhs_scale=moving[1],
                 start=start,
                 stop=stop,
             )
 
-        def both(grouped):
-            return grouped[:].rearrange("p e m j -> p (e m j)")
+        w1_dealt = [deal_pair(f"w1_dealt{u}", w1_raw, u) for u in range(2)]
+        w2_dealt = [deal_pair(f"w2_dealt{u}", w2_raw, u) for u in range(2)]
 
-        def one(grouped, e):
-            return grouped[:, e, :, :].rearrange("p m j -> p (m j)")
-
-        w1_g = [deal_pair(f"w1_g{u}", w1_raw, u) for u in range(2)]
-        w2_g = [deal_pair(f"w2_g{u}", w2_raw, u) for u in range(2)]
-
-        x_cd = [keep.tile([P, S], U32, name=f"x_cd{i}", align_bytes=64) for i in range(2)]
+        picked_scales = [keep.tile([P, S], U8, name=f"picked_scales{i}", align_bytes=64) for i in range(3)]
         for i in range(3):
-            gather_scales(i)
-        gather_words(0)
-        gather_words(1)
-        w1_q = [quantize("w1_0", both(w1_g[0]), 2 * P)]
-        x_cd.append(keep.tile([P, S], U32, name="x_cd2", tag="w1_g0", align_bytes=64))
-        gather_words(2)
-        w2_q = [quantize(f"w2_{e}", one(w2_g[0], e), P) for e in range(2)]
-        w1_q.append(quantize("w1_1", both(w1_g[1]), 2 * P, tag="w2_g0"))
-        w2_q.extend(quantize(f"w2_{2 + e}", one(w2_g[1], e), P) for e in range(2))
+            nc.vector.tensor_copy(picked_scales[i][:], table_scales[:].indirect(lists[i][:]))
+        w1_pairs = [quantize_pair("w1_pair0", w1_dealt[0])]
+        picked_words = keep.tile([P, 3, S], U32, name="picked_words", tag="w1_dealt0", align_bytes=64)
+        for i in range(3):
+            nc.vector.tensor_copy(picked_words[:, i, :], table_words[:].bitcast(U32).indirect(lists[i][:]))
+        picked = [(picked_words[:, i, :], picked_scales[i][:]) for i in range(3)]
+        w2_planes = [quantize_plane(f"w2_plane{e}", w2_dealt[0], e) for e in range(2)]
+        w1_pairs.append(quantize_pair("w1_pair1", w1_dealt[1], tag="w2_dealt0"))
+        w2_planes.extend(quantize_plane(f"w2_plane{2 + e}", w2_dealt[1], e) for e in range(2))
 
         y_acc = [psum.tile([P, S], F32, name=f"y{t}", tag=f"bank{2 * t}") for t in range(PACK)]
         e_acc = [psum.tile([P, S], F32, name=f"e{t}", tag=f"bank{2 * t + 1}") for t in range(PACK)]
-
-        def first_pass(t):
-            cols = slice(P * (t % 2), P * (t % 2) + P)
-            mm(y_acc[t][:], w1_q[t // 2], cols, x_cd[0][:], x_sc[0][:], True, False)
-            mm(e_acc[t][:], w1_q[t // 2], cols, x_cd[1][:], x_sc[1][:], True, False)
-
-        def second_pass(t):
-            mm(e_acc[t][:], w2_q[t], slice(0, P), x_cd[2][:], x_sc[2][:], False, True)
-            mm(y_acc[t][:], w2_q[t], slice(0, P), x_cd[1][:], x_sc[1][:], False, True)
-
-        for rep in range(3):
-            mm(y_acc[3][:], (x_cd[0], x_sc[0]), slice(0, P), x_cd[0][:], x_sc[0][:], True, True)
-        first_pass(0)
-        first_pass(1)
-        second_pass(0)
-        second_pass(1)
+        for t in (0, 1):
+            product(y_acc[t][:], w1_pairs[0], t, picked[0], True, False)
+            product(e_acc[t][:], w1_pairs[0], t, picked[1], True, False)
+        for t in (0, 1):
+            product(e_acc[t][:], w2_planes[t], 0, picked[2], False, True)
+            product(y_acc[t][:], w2_planes[t], 0, picked[1], False, True)
         for t in (2, 3):
-            first_pass(t)
-            second_pass(t)
+            for acc, place in ((e_acc[t], 1), (y_acc[t], 0)):
+                product(acc[:], w1_pairs[1], t - 2, picked[place], True, False)
+                product(acc[:], w2_planes[t], 0, picked[place + 1], False, True)
 
         own = keep.tile([P, PACK, S], F32, name="own")
         window = [keep.tile([P, S], F32, name=f"window{t}") for t in range(PACK)]
         e_sb = [keep.tile([P, S], F32, name=f"e_sb{t}", tag=f"e_sb{t}", align_bytes=64) for t in range(PACK)]
         larger = [keep.tile([P, S], F32, name=f"larger{t}", tag=f"larger{t}", align_bytes=64) for t in range(PACK)]
-        mx = [keep.tile([P, S], F32, name=f"mx{t}", tag=f"mx{t}") for t in range(PACK)]
-        early = keep.tile([P, PACK, HALF], F32, name="early")
+        mx = [keep.tile([P, S], F32, name=f"mx{t}", align_bytes=64) for t in range(PACK)]
+        sums_front = keep.tile([P, PACK, HALF], F32, name="sums_front")
 
         def take_larger(t):
             nc.scalar.copy(e_sb[t][:], e_acc[t][:])
             nc.vector.tensor_tensor(larger[t][:], y_acc[t][:], e_sb[t][:], ALU.max)
 
+        def scale_own(t, j0):
+            cols = slice(j0, j0 + HALF)
+            nc.scalar.activation(own[:, t, cols], mx[t][:, cols], ACT.Copy, scale=gain[:, t : t + 1])
+
         def add_mates(dst, t, j0, n):
-            cols = slice(j0 // LIST_ROWS, (j0 + n) // LIST_ROWS)
-            nc.vector.tensor_tensor(
-                dst, window[t][:].indirect(mate_list[:, cols]), own[:, t, j0 : j0 + n], ALU.add
-            )
+            entries = mate_list[:, j0 // LIST_GROUP : (j0 + n) // LIST_GROUP]
+            nc.vector.tensor_tensor(dst, window[t][:].indirect(entries), own[:, t, j0 : j0 + n], ALU.add)
 
         def activate(t):
-            nc.scalar.activation(mx[t][:], larger[t][:], ACT.Tanh)
-            nc.scalar.activation(own[:, t, :], mx[t][:], ACT.Copy, scale=gain[:, t : t + 1])
+            nc.scalar.activation(mx[t][:], larger[t][:], ACT.Tanh, bias=no_bias[:])
+            scale_own(t, 0)
             nc.vector.tensor_scalar(window[t][:], mx[t][:], gain[:, t : t + 1], None, ALU.mult)
-            add_mates(early[:, t, :], t, 0, HALF)
+            add_mates(sums_front[:, t, :], t, 0, HALF)
 
-        def group_w3(h, tag, copy, parts):
-            grouped = keep.tile([P, HALF, PACK], BF16, name=f"w3_g{h}", tag=tag, align_bytes=64)
-            dst = grouped[:].rearrange("p (c i) j -> p c j i", i=4)
-            src = w3_raw[:, :, HALF * h : HALF * h + HALF].rearrange("p j (c i) -> p c j i", i=4)
-            step = HALF // 4 // parts
-            for c0 in range(0, HALF // 4, step):
+        def weave(name, tag, rows, width, copy, pieces):
+            woven = keep.tile([P, width, PACK], BF16, name=name + "_woven", tag=tag, align_bytes=64)
+            dst = woven[:].rearrange("p (c i) j -> p c j i", i=LINE)
+            src = rows.rearrange("p j (c i) -> p c j i", i=LINE)
+            step = width // LINE // pieces
+            for c0 in range(0, width // LINE, step):
                 copy(dst[:, c0 : c0 + step], src[:, c0 : c0 + step])
-            return quantize(f"w3_{h}", grouped[:].rearrange("p c j -> p (c j)"), HALF)
+            return quantize(name, woven[:].rearrange("p c j -> p (c j)"), width)
 
-        w3_q = [group_w3(0, "w2_g1", nc.vector.tensor_copy, 1)]
+        w3_halves = [weave("w3_half0", "w1_dealt1", w3_raw[:, :, : N // 2], N // 2, nc.vector.tensor_copy, 1)]
+
         take_larger(0)
-        take_larger(1)
-        activate(0)
-        take_larger(2)
-        activate(1)
-        take_larger(3)
-        activate(2)
-        activate(3)
-        w3_q.append(group_w3(1, "larger3", nc.scalar.copy, 1))
+        for t in range(1, PACK):
+            take_larger(t)
+            activate(t - 1)
+        activate(PACK - 1)
+        for t in range(PACK):
+            scale_own(t, HALF)
+
         out_rows = out.rearrange("(r p) j -> p r j", p=P)
 
-        def finish(c, sums, weave, second_copy):
-            z = keep.tile([P, CHUNK, PACK], BF16, name=f"z{c}", tag=f"z{c}", align_bytes=64)
-            weave(
-                z[:].rearrange("p (c i) t -> p c t i", i=4),
-                sums.rearrange("p t (c i) -> p c t i", i=4),
-            )
-            z_q = quantize(f"z{c}", z[:].rearrange("p c t -> p (c t)"), CHUNK)
-            for h, copy in enumerate((nc.scalar.copy, second_copy)):
-                acc = psum.tile([P, 2, CHUNK], F32, name=f"o{c}_{h}", tag=f"bank{2 * c + h}")
-                for r in range(2):
-                    mm(acc[:, r, :], w3_q[h], slice(P * r, P * r + P), z_q[0][:], z_q[1][:], True, True)
-                res = keep.tile([P, 2, CHUNK], F32, name=f"res{c}_{h}")
-                copy(res[:], acc[:])
-                nc.sync.dma_start(out_rows[:, 2 * h : 2 * h + 2, CHUNK * c : CHUNK * c + CHUNK], res[:])
+        def weave_chunk(c, sums, copy):
+            words, scales = weave(f"z{c}", f"z{c}", sums, CHUNK, copy, 1)
+            return words[:], scales[:]
 
-        finish(0, early[:, :, :CHUNK], nc.scalar.copy, nc.scalar.copy)
-        finish(1, early[:, :, CHUNK:], nc.scalar.copy, nc.scalar.copy)
-        late = [
-            keep.tile([P, PACK, CHUNK], F32, name="late0", tag="mx3"),
-            keep.tile([P, PACK, CHUNK], F32, name="late1", tag="z0", align_bytes=64),
+        def last_layer(c, h, copy):
+            acc = psum.tile([P, 2, CHUNK], F32, name=f"out{c}_{h}", tag=f"bank{2 * c + h}")
+            for r in range(2):
+                product(acc[:, r, :], w3_halves[h], r, z_chunks[c], True, True)
+            result = keep.tile([P, 2, CHUNK], F32, name=f"result{c}_{h}")
+            copy(result[:], acc[:])
+            nc.sync.dma_start(out_rows[:, 2 * h : 2 * h + 2, CHUNK * c : CHUNK * c + CHUNK], result[:])
+
+        z_chunks = [
+            weave_chunk(c, sums_front[:, :, CHUNK * c : CHUNK * c + CHUNK], nc.scalar.copy) for c in range(2)
         ]
-        for c in range(2):
-            for t in range(PACK):
-                add_mates(late[c][:, t, :], t, HALF + CHUNK * c, CHUNK)
-        finish(2, late[0][:], nc.scalar.copy, nc.scalar.copy)
-        finish(3, late[1][:], nc.vector.tensor_copy, nc.vector.tensor_copy)
+        w3_halves.append(weave("w3_half1", "e_sb1", w3_raw[:, :, N // 2 :], N // 2, nc.scalar.copy, 2))
+
+        sums_back = [
+            keep.tile([P, PACK, CHUNK], F32, name="sums_chunk2", tag="larger3", align_bytes=64),
+            keep.tile([P, PACK, CHUNK], F32, name="sums_chunk3", tag="z0", align_bytes=64),
+        ]
+        for t in range(PACK):
+            add_mates(sums_back[0][:, t, :], t, HALF, CHUNK)
+        z_chunks.append(weave_chunk(2, sums_back[0][:], nc.scalar.copy))
+        for h in range(2):
+            for c in range(2):
+                last_layer(c, h, nc.scalar.copy)
+        for t in range(PACK):
+            add_mates(sums_back[1][:, t, :], t, HALF + CHUNK, CHUNK)
+        z_chunks.append(weave_chunk(3, sums_back[1][:], nc.vector.tensor_copy))
+        last_layer(2, 0, nc.scalar.copy)
+        last_layer(2, 1, nc.scalar.copy)
+        last_layer(3, 0, nc.scalar.copy)
+        last_layer(3, 1, nc.vector.tensor_copy)

from contextlib import ExitStack

import concourse.mybir as mybir

K, T, S, N, H = 512, 2048, 512, 512, 512
FLOPS = 2 * S * (4 * K * H + H * N)

F32 = mybir.dt.float32
BF16 = mybir.dt.bfloat16
I32 = mybir.dt.int32
U32 = mybir.dt.uint32
U16 = mybir.dt.uint16
U8 = mybir.dt.uint8
FP8X4 = mybir.dt.float8_e4m3fn_x4
ALU = mybir.AluOpType
ACT = mybir.ActivationFunctionType

P = 128
PACK = 4
QUADRANT = 32
LIST_GROUP = 16
LINE = 4
HALF = S // 2
CHUNK = S // 4


def tile_picked_charcnn_tanh_p_kernel(
    tc, x_words, x_scales, w1, w2, gn, w3, offs, c1, c2, mate, out
):
    nc = tc.nc
    with ExitStack() as ctx:
        keep = ctx.enter_context(tc.tile_pool(name="keep", bufs=1))
        psum = ctx.enter_context(tc.psum_pool(name="psum", bufs=1))

        def load_list(name, src):
            tile = keep.tile([P, S // LIST_GROUP], U16, name=name)
            nc.sync.dma_start(tile[:], src)
            return tile

        def weight_rows(w):
            return w.rearrange("(p j) c -> p j c", j=PACK)

        def load_weight(name, w):
            tile = keep.tile([P, PACK, w.shape[1]], F32, name=name)
            nc.sync.dma_start(tile[:], weight_rows(w))
            return tile

        table_scales = keep.tile([P, T], U8, name="table_scales")
        nc.vector.memset(table_scales[:].bitcast(I32), 0)

        zero = keep.tile([P, 1], F32, name="zero")
        no_bias = keep.tile([P, 1], F32, name="no_bias")
        nc.vector.memset(zero[:], 0.0)
        nc.scalar.activation(no_bias[:], zero[:], ACT.Tanh)

        lists = [load_list("offs_list", offs), load_list("c1_list", c1)]
        w1_raw = keep.tile([P, PACK, H], F32, name="w1_raw")
        nc.sync.dma_start(w1_raw[:, :1], weight_rows(w1)[:, :1])
        for q in range(P // QUADRANT):
            nc.sync.dma_start(
                table_scales[QUADRANT * q : QUADRANT * q + 4, :].bitcast(I32),
                x_scales[0, 4 * q : 4 * q + 4, :].bitcast(I32),
            )
        nc.sync.dma_start(w1_raw[:, 1:], weight_rows(w1)[:, 1:])
        lists.append(load_list("c2_list", c2))
        table_words = keep.tile([P, T], I32, name="table_words")
        nc.sync.dma_start(table_words[:], x_words[0].rearrange("p n j -> p (n j)").bitcast(I32))
        w2_raw = load_weight("w2_raw", w2)
        w3_raw = load_weight("w3_raw", w3)
        mate_list = load_list("mate_list", mate)
        gain = keep.tile([P, PACK], F32, name="gain")
        nc.sync.dma_start(gain[:], gn.rearrange("(p t) o -> p (t o)", t=PACK))

        def deal_pair(name, raw, u):
            dealt = keep.tile([P, 2, P, PACK], BF16, name=name, tag=name, align_bytes=64)
            nc.scalar.copy(
                dealt[:].rearrange("p e m j -> p m j e"),
                raw[:].rearrange("p j (m u e) -> p u m j e", u=2, e=2)[:, u],
            )
            return dealt

        def quantize(name, values, width, tag=None):
            words = keep.tile([P, width], U32, name=name + "_words", tag=tag or name + "_words", align_bytes=64)
            scales = keep.tile([P, width], U8, name=name + "_scales", align_bytes=64)
            nc.vector.quantize_mx(words[:].bitcast(FP8X4), scales[:], values)
            return words, scales

        def quantize_pair(name, dealt, tag=None):
            return quantize(name, dealt[:].rearrange("p e m j -> p (e m j)"), 2 * P, tag)

        def quantize_plane(name, dealt, e):
            return quantize(name, dealt[:, e, :, :].rearrange("p m j -> p (m j)"), P)

        def product(acc, weights, block, moving, start, stop):
            cols = slice(P * block, P * block + P)
            nc.tensor.matmul_mx(
                out=acc,
                lhsT=weights[0][:, cols].bitcast(FP8X4),
                lhsT_scale=weights[1][:, cols],
                rhs=moving[0].bitcast(FP8X4),
                rhs_scale=moving[1],
                start=start,
                stop=stop,
            )

        w1_dealt = [deal_pair(f"w1_dealt{u}", w1_raw, u) for u in range(2)]
        w2_dealt = [deal_pair(f"w2_dealt{u}", w2_raw, u) for u in range(2)]

        picked_scales = [keep.tile([P, S], U8, name=f"picked_scales{i}", align_bytes=64) for i in range(3)]
        for i in range(3):
            nc.vector.tensor_copy(picked_scales[i][:], table_scales[:].indirect(lists[i][:]))
        w1_pairs = [quantize_pair("w1_pair0", w1_dealt[0])]
        picked_words = keep.tile([P, 3, S], U32, name="picked_words", tag="w1_dealt0", align_bytes=64)
        for i in range(3):
            nc.vector.tensor_copy(picked_words[:, i, :], table_words[:].bitcast(U32).indirect(lists[i][:]))
        picked = [(picked_words[:, i, :], picked_scales[i][:]) for i in range(3)]
        w2_planes = [quantize_plane(f"w2_plane{e}", w2_dealt[0], e) for e in range(2)]
        w1_pairs.append(quantize_pair("w1_pair1", w1_dealt[1], tag="w2_dealt0"))
        w2_planes.extend(quantize_plane(f"w2_plane{2 + e}", w2_dealt[1], e) for e in range(2))

        y_acc = [psum.tile([P, S], F32, name=f"y{t}", tag=f"bank{2 * t}") for t in range(PACK)]
        e_acc = [psum.tile([P, S], F32, name=f"e{t}", tag=f"bank{2 * t + 1}") for t in range(PACK)]
        for t in (0, 1):
            product(y_acc[t][:], w1_pairs[0], t, picked[0], True, False)
            product(e_acc[t][:], w1_pairs[0], t, picked[1], True, False)
        for t in (0, 1):
            product(e_acc[t][:], w2_planes[t], 0, picked[2], False, True)
            product(y_acc[t][:], w2_planes[t], 0, picked[1], False, True)
        for t in (2, 3):
            for acc, place in ((e_acc[t], 1), (y_acc[t], 0)):
                product(acc[:], w1_pairs[1], t - 2, picked[place], True, False)
                product(acc[:], w2_planes[t], 0, picked[place + 1], False, True)

        own = keep.tile([P, PACK, S], F32, name="own")
        window = [keep.tile([P, S], F32, name=f"window{t}") for t in range(PACK)]
        e_sb = [keep.tile([P, S], F32, name=f"e_sb{t}", tag=f"e_sb{t}", align_bytes=64) for t in range(PACK)]
        larger = [keep.tile([P, S], F32, name=f"larger{t}", tag=f"larger{t}", align_bytes=64) for t in range(PACK)]
        mx = [keep.tile([P, S], F32, name=f"mx{t}", align_bytes=64) for t in range(PACK)]
        sums_front = keep.tile([P, PACK, HALF], F32, name="sums_front")

        def take_larger(t):
            nc.scalar.copy(e_sb[t][:], e_acc[t][:])
            nc.vector.tensor_tensor(larger[t][:], y_acc[t][:], e_sb[t][:], ALU.max)

        def scale_own(t, j0):
            cols = slice(j0, j0 + HALF)
            nc.scalar.activation(own[:, t, cols], mx[t][:, cols], ACT.Copy, scale=gain[:, t : t + 1])

        def add_mates(dst, t, j0, n):
            entries = mate_list[:, j0 // LIST_GROUP : (j0 + n) // LIST_GROUP]
            nc.vector.tensor_tensor(dst, window[t][:].indirect(entries), own[:, t, j0 : j0 + n], ALU.add)

        def activate(t):
            nc.scalar.activation(mx[t][:], larger[t][:], ACT.Tanh, bias=no_bias[:])
            scale_own(t, 0)
            nc.vector.tensor_scalar(window[t][:], mx[t][:], gain[:, t : t + 1], None, ALU.mult)
            add_mates(sums_front[:, t, :], t, 0, HALF)

        def weave(name, tag, rows, width, copy, pieces):
            woven = keep.tile([P, width, PACK], BF16, name=name + "_woven", tag=tag, align_bytes=64)
            dst = woven[:].rearrange("p (c i) j -> p c j i", i=LINE)
            src = rows.rearrange("p j (c i) -> p c j i", i=LINE)
            step = width // LINE // pieces
            for c0 in range(0, width // LINE, step):
                copy(dst[:, c0 : c0 + step], src[:, c0 : c0 + step])
            return quantize(name, woven[:].rearrange("p c j -> p (c j)"), width)

        w3_halves = [weave("w3_half0", "w1_dealt1", w3_raw[:, :, : N // 2], N // 2, nc.vector.tensor_copy, 1)]

        take_larger(0)
        for t in range(1, PACK):
            take_larger(t)
            activate(t - 1)
        activate(PACK - 1)
        for t in range(PACK):
            scale_own(t, HALF)

        out_rows = out.rearrange("(r p) j -> p r j", p=P)

        def weave_chunk(c, sums, copy):
            words, scales = weave(f"z{c}", f"z{c}", sums, CHUNK, copy, 1)
            return words[:], scales[:]

        def last_layer(c, h, copy):
            acc = psum.tile([P, 2, CHUNK], F32, name=f"out{c}_{h}", tag=f"bank{2 * c + h}")
            for r in range(2):
                product(acc[:, r, :], w3_halves[h], r, z_chunks[c], True, True)
            result = keep.tile([P, 2, CHUNK], F32, name=f"result{c}_{h}")
            copy(result[:], acc[:])
            nc.sync.dma_start(out_rows[:, 2 * h : 2 * h + 2, CHUNK * c : CHUNK * c + CHUNK], result[:])

        z_chunks = [
            weave_chunk(c, sums_front[:, :, CHUNK * c : CHUNK * c + CHUNK], nc.scalar.copy) for c in range(2)
        ]
        w3_halves.append(weave("w3_half1", "e_sb1", w3_raw[:, :, N // 2 :], N // 2, nc.scalar.copy, 2))

        sums_back = [
            keep.tile([P, PACK, CHUNK], F32, name="sums_chunk2", tag="larger3", align_bytes=64),
            keep.tile([P, PACK, CHUNK], F32, name="sums_chunk3", tag="z0", align_bytes=64),
        ]
        for t in range(PACK):
            add_mates(sums_back[0][:, t, :], t, HALF, CHUNK)
        z_chunks.append(weave_chunk(2, sums_back[0][:], nc.scalar.copy))
        for h in range(2):
            for c in range(2):
                last_layer(c, h, nc.scalar.copy)
        for t in range(PACK):
            add_mates(sums_back[1][:, t, :], t, HALF + CHUNK, CHUNK)
        z_chunks.append(weave_chunk(3, sums_back[1][:], nc.vector.tensor_copy))
        last_layer(2, 0, nc.scalar.copy)
        last_layer(2, 1, nc.scalar.copy)
        last_layer(3, 0, nc.scalar.copy)
        last_layer(3, 1, nc.vector.tensor_copy)
